import numpy as np
import ml_dtypes


def mxq(x, axis, fmt="e4m3"):
    dtype, down = {"e4m3": (ml_dtypes.float8_e4m3fn, 7), "e5m2": (ml_dtypes.float8_e5m2, 14)}[fmt]
    v = np.moveaxis(np.asarray(x, np.float32).astype(ml_dtypes.bfloat16).astype(np.float64), axis, -1)
    blocks = v.reshape(v.shape[:-1] + (-1, 32))
    amax = np.abs(blocks).max(-1, keepdims=True)
    byte = np.maximum(np.where(amax > 0, np.frexp(amax)[1] - 1 + 127, 0) - down, 1)
    scale = np.exp2(byte - 127.0)
    codes = (blocks / scale).astype(np.float32).astype(dtype).astype(np.float64)
    return np.moveaxis((codes * scale).reshape(v.shape), -1, axis)


WIDE = False


def mx_kscale(k):
    if not WIDE:
        return np.ones(k)
    levels = np.array([10, -10, 5, -5, 0])
    if k % 512:
        return np.exp2(np.random.permutation(np.resize(levels, k // 32))).repeat(32)
    a = np.empty((k // 512, 16))
    for p in range(k // 512):
        a[p, :8] = np.random.permutation(np.resize(levels, 8))
        for g in range(8):
            far = levels[np.abs(levels - a[p, g]) >= 10]
            a[p, g + 8] = far[np.random.randint(len(far))]
    return np.exp2(a.ravel()).repeat(32)


def f64(x):
    return np.asarray(x).astype(np.float64)


def striped(idx):
    return np.tile(idx.reshape(-1, 16).T, (8, 1)).astype(np.uint16)


def unstriped(offs):
    return offs[:16].T.reshape(-1).astype(np.int64)


def striped8(idx):
    return np.concatenate([x.reshape(-1, 16).T for x in idx]).astype(np.uint16)


def runs(offs, k):
    lists = np.stack([offs[16 * r : 16 * r + 16].T.reshape(-1) for r in range(8)]).astype(np.int64)
    return lists[np.arange(k) % 512 // 64]


def pack_weight(w):
    k, n = w.shape
    w = f64(np.asarray(w, np.float32).astype(ml_dtypes.bfloat16)).reshape(k // 32, 32, n)
    amax = np.abs(w).max(1)
    byte = np.clip(np.where(amax > 0, np.frexp(amax)[1] - 1 + 127 - 7, 1), 1, 254)
    scaled = (w * np.exp2(127.0 - byte)[:, None, :]).reshape(k, n).astype(np.float32)
    words = np.ascontiguousarray(scaled.reshape(k // 512, 128, 4, n).transpose(0, 1, 3, 2)).astype(ml_dtypes.float8_e4m3fn).view(np.uint8)
    return words, np.ascontiguousarray(byte.astype(np.uint8).reshape(k // 512, 16, n))


def unpack_weight(words, scales):
    g, p, n, _ = words.shape
    vals = np.ascontiguousarray(words).view(ml_dtypes.float8_e4m3fn).astype(np.float64) * np.repeat(np.exp2(scales.astype(np.float64) - 127.0), 8, axis=1)[..., None]
    return vals.transpose(0, 1, 3, 2).reshape(g * 512, n)


def relu(v):
    return np.maximum(v, 0.0)

def planes(y):
    n, m = y.shape
    v = y.astype(np.float32).astype(ml_dtypes.bfloat16).astype(np.float64).reshape(n // 32, 32, m)
    top = np.abs(v).max(1)
    byte = np.clip(np.where(top > 0, np.frexp(top)[1] - 1 + 127 - 7, 1), 1, 254)
    codes = (v * np.exp2(127.0 - byte)[:, None, :]).reshape(n, m).astype(np.float32).astype(ml_dtypes.float8_e4m3fn).view(np.uint8)
    words = codes.reshape(n // 512, 128, 4, m).transpose(0, 1, 3, 2)
    return np.ascontiguousarray(words), np.ascontiguousarray(byte.astype(np.uint8).reshape(n // 512, 16, m))


K, T, S, N, H, W, U = 512, 2048, 512, 512, 512, 256, 1024


def setup_inputs():
    n = np.random.standard_normal
    s = mx_kscale(K)[:, None]
    u = mx_kscale(S)
    packed_xT = pack_weight(n((K, T)) * s)
    perm = np.stack([np.random.permutation(H) for _ in range(8)])
    return {
        "x_words": packed_xT[0],
        "x_scales": packed_xT[1],
        "wa": (n((K, H)) / np.sqrt(K) / s).astype(np.float32),
        "wb": (n((K, N)) / np.sqrt(K) / s).astype(np.float32),
        "gt": (np.random.uniform(0.5, 1.5, (S, 1)) * u[:, None]).astype(np.float32),
        "gi": (np.random.uniform(0.5, 1.5, (S, 1)) / u[:, None]).astype(np.float32),
        "offs": striped(np.random.permutation(T)[:S]),
        "two": striped(np.random.permutation(T)[:S]),
        "n1": striped8(perm[:, :W]),
        "n2": striped8(perm[:, W:]),
        "n3": striped8(np.stack([np.random.permutation(H) for _ in range(8)])),
        "n4": striped8(np.stack([np.random.permutation(U)[:N] for _ in range(8)])),
        "n5": striped8(np.stack([np.random.permutation(N) for _ in range(8)])),
    }


def reference(x_words, x_scales, wa, wb, gt, gi, offs, two, n1, n2, n3, n4, n5):
    xq = unpack_weight(x_words, x_scales)[:, unstriped(offs)]
    a = xq.T @ mxq(f64(wa), 0, "e4m3")
    pa = a[np.arange(S)[:, None], runs(n1, S)]
    pb = a[np.arange(S)[:, None], runs(n2, S)]
    ra = pa - (0.5 * pb)
    ds = a.copy()
    ds[np.arange(S)[:, None], runs(n2, S)] = ra
    z = f64(gt) * (ds - (0.5 * (ds[np.arange(S)[:, None], runs(n3, S)])))
    x_two = unpack_weight(x_words, x_scales)[:, unstriped(two)]
    b = x_two.T @ mxq(f64(wb), 0, "e4m3")
    z2 = f64(gi) * b
    cv = 0.0625 * ((mxq(z, 0, "e4m3").T @ mxq(z2, 0, "e4m3")))
    nw = cv - (relu(cv[np.arange(H)[:, None], runs(n5, H)]))
    out = np.zeros((H, U))
    out[np.arange(H)[:, None], runs(n4, H)] = nw
    return (out,) + planes(out)

@@ -1,0 +1,273 @@
+from contextlib import ExitStack
+
+import concourse.mybir as mybir
+from concourse.masks import make_identity
+
+K, T, S, N, H, W, U = 512, 2048, 512, 512, 512, 256, 1024
+FLOPS = 3 * 2 * 512 * 512 * 512
+
+F32 = mybir.dt.float32
+BF16 = mybir.dt.bfloat16
+I32 = mybir.dt.int32
+U32 = mybir.dt.uint32
+U16 = mybir.dt.uint16
+U8 = mybir.dt.uint8
+FP8X4 = mybir.dt.float8_e4m3fn_x4
+MULT = mybir.AluOpType.mult
+ADD = mybir.AluOpType.add
+SUB = mybir.AluOpType.subtract
+COPY = mybir.ActivationFunctionType.Copy
+RELU = mybir.ActivationFunctionType.Relu
+
+P = 128
+PACK = 4
+HALF = 256
+
+
+def tile_picked_momfolddpagez_none_po_kernel(
+    tc, x_words, x_scales, wa, wb, gt, gi, offs, two, n1, n2, n3, n4, n5, out_0, out_1, out_2
+):
+    nc = tc.nc
+    with ExitStack() as ctx:
+        keep = ctx.enter_context(tc.tile_pool(name="keep", bufs=1))
+        psum = ctx.enter_context(tc.psum_pool(name="psum", bufs=1))
+
+        def load_list(src, name):
+            lst = keep.tile([P, src.shape[1]], U16, name=name)
+            nc.sync.dma_start(lst[:], src)
+            return lst
+
+        def load_weight_half(w, h, name):
+            raw = keep.tile([P, PACK, HALF], F32, name=name)
+            nc.sync.dma_start(raw[:], w.rearrange("(p j) c -> p j c", j=PACK)[:, :, h * HALF : (h + 1) * HALF])
+            return raw
+
+        def weave(dst, src):
+            nc.scalar.copy(
+                dst.rearrange("p (c i) j -> p c j i", i=4),
+                src.rearrange("p j (c i) -> p c j i", i=4),
+            )
+
+        def quantize(codes, scales, src):
+            nc.vector.quantize_mx(out=codes.bitcast(FP8X4), scales=scales, in_=src)
+
+        def product(acc, l_codes, l_scales, r_codes, r_scales):
+            nc.tensor.matmul_mx(
+                out=acc, lhsT=l_codes.bitcast(FP8X4), lhsT_scale=l_scales,
+                rhs=r_codes.bitcast(FP8X4), rhs_scale=r_scales, start=True, stop=True,
+            )
+
+        xs = keep.tile([P, T], U8, name="xs")
+        nc.vector.memset(xs[:].bitcast(I32), 0)
+        offs_t = load_list(offs, "offs_t")
+        two_t = load_list(two, "two_t")
+        wa_raw = [load_weight_half(wa, 0, "wa_raw0")]
+        for q in range(4):
+            nc.sync.dma_start(xs[32 * q : 32 * q + 4, :].bitcast(I32), x_scales[0, 4 * q : 4 * q + 4, :].bitcast(I32))
+        wa_raw.append(load_weight_half(wa, 1, "wa_raw1"))
+        xw = keep.tile([P, T], I32, name="xw")
+        nc.sync.dma_start(xw[:], x_words[0].rearrange("p c r -> p (c r)").bitcast(I32))
+
+        grow = keep.tile([P, P], F32, name="grow")
+        nc.gpsimd.memset(grow[:], 0.0)
+        ident = keep.tile([P, P], F32, name="ident")
+        make_identity(nc, ident[:])
+        for row, g in ((0, gt), (PACK, gi)):
+            nc.sync.dma_start(
+                grow[row : row + PACK, :].rearrange("t (b r) -> t b r", r=8),
+                g.rearrange("(b t r) one -> t b (r one)", t=PACK, r=8),
+            )
+        n1_t = load_list(n1, "n1_t")
+        n2_t = load_list(n2, "n2_t")
+        wb_raw = [load_weight_half(wb, h, "wb_raw%d" % h) for h in range(2)]
+        n3_t = load_list(n3, "n3_t")
+        n5_t = load_list(n5, "n5_t")
+        n4_t = load_list(n4, "n4_t")
+
+        pages = [keep.tile([P, U], F32, name="page%d" % t) for t in range(PACK - 1)]
+        for page in pages:
+            nc.vector.memset(page[:], 0.0)
+
+        def pick_scales(lst, name):
+            got = keep.tile([P, S], U8, name=name + "_got")
+            nc.vector.tensor_copy(got[:], xs[:].indirect(lst[:]))
+            dealt = keep.tile([P, S], U8, name=name, align_bytes=64)
+            nc.vector.tensor_copy(
+                dealt[:].bitcast(I32).rearrange("p (t b w) -> p t b w", t=PACK, w=2),
+                got[:].bitcast(I32).rearrange("p (b t w) -> p t b w", t=PACK, w=2),
+            )
+            return dealt
+
+        def pick_words(lst, name):
+            dealt = keep.tile([P, S], U32, name=name, align_bytes=64)
+            nc.vector.tensor_copy(
+                dealt[:].rearrange("p (t b r) -> p b t r", t=PACK, r=8), xw[:].bitcast(U32).indirect(lst[:])
+            )
+            return dealt
+
+        xa_s = pick_scales(offs_t, "xa_s")
+        xb_s = pick_scales(two_t, "xb_s")
+
+        wa_c = keep.tile([P, H], U32, name="wa_c", align_bytes=64)
+        wa_s = keep.tile([P, H], U8, name="wa_s", align_bytes=64)
+        for h in range(2):
+            woven = keep.tile([P, HALF, PACK], BF16, name="wa_w%d" % h, align_bytes=64)
+            weave(woven[:], wa_raw[h][:])
+            cols = slice(h * HALF, (h + 1) * HALF)
+            quantize(wa_c[:, cols], wa_s[:, cols], woven[:].rearrange("p c j -> p (c j)"))
+
+        xa_c = pick_words(offs_t, "xa_c")
+        xb_c = pick_words(two_t, "xb_c")
+
+        gT = psum.tile([P, P], F32, name="gT", tag="bank7")
+        nc.tensor.transpose(gT[:], grow[:], ident[:])
+        gcol = keep.tile([P, 2 * PACK], F32, name="gcol")
+        nc.scalar.activation(gcol[:, 0:PACK], gT[:, 0:PACK], COPY, scale=-0.5)
+        nc.scalar.copy(gcol[:, PACK : 2 * PACK], gT[:, PACK : 2 * PACK])
+
+        ds = []
+        aw = []
+        a_accs = []
+
+        def second(t):
+            d = keep.tile([P, H], F32, name="ds%d" % t)
+            nc.scalar.activation(d[:], a_accs[t][:], COPY, scale=gcol[:, t : t + 1])
+            ds.append(d)
+
+        for t in range(PACK):
+            acc = psum.tile([P, H], F32, name="a_acc%d" % t, tag="bank%d" % t)
+            cols = slice(t * P, (t + 1) * P)
+            product(acc[:], xa_c[:, cols], xa_s[:, cols], wa_c[:], wa_s[:])
+            d = keep.tile([P, H], F32, name="aw%d" % t)
+            nc.scalar.activation(d[:], acc[:], COPY, scale=gcol[:, t : t + 1])
+            aw.append(d)
+            a_accs.append(acc)
+            if t > 0:
+                second(t - 1)
+        second(PACK - 1)
+
+        wb_c = keep.tile([P, N], U32, name="wb_c", align_bytes=64)
+        wb_s = keep.tile([P, N], U8, name="wb_s", align_bytes=64)
+        for h in range(2):
+            woven = keep.tile([P, HALF, PACK], BF16, name="wb_w%d" % h, tag="wb_w%d" % h, align_bytes=64)
+            weave(woven[:], wb_raw[h][:])
+            cols = slice(h * HALF, (h + 1) * HALF)
+            quantize(wb_c[:, cols], wb_s[:, cols], woven[:].rearrange("p c j -> p (c j)"))
+        z2f = keep.tile([P, PACK, N], F32, name="z2f")
+        for t in range(PACK):
+            acc = psum.tile([P, N], F32, name="b_acc%d" % t, tag="bank%d" % (PACK + t))
+            cols = slice(t * P, (t + 1) * P)
+            product(acc[:], xb_c[:, cols], xb_s[:, cols], wb_c[:], wb_s[:])
+            nc.scalar.activation(z2f[:, t, :], acc[:], COPY, scale=gcol[:, PACK + t : PACK + t + 1])
+        z2w = keep.tile([P, N, PACK], BF16, name="z2w", align_bytes=64)
+        weave(z2w[:], z2f[:])
+        z2_c = keep.tile([P, N], U32, name="z2_c", align_bytes=64)
+        z2_s = keep.tile([P, N], U8, name="z2_s", align_bytes=64)
+        quantize(z2_c[:], z2_s[:], z2w[:].rearrange("p c j -> p (c j)"))
+
+        pa_tags = ["pa0", "pa1", "pa2", "zf"]
+        pb_tags = ["pb0", "pb1", "pb2", "wb_w1"]
+        twice = []
+        pab = []
+
+        def fold(t):
+            nc.vector.tensor_tensor(ds[t][:].indirect(n2_t[:]), pab[t][0][:], pab[t][1][:], ADD)
+            tw = keep.tile([P, H], F32, name="twice%d" % t)
+            nc.scalar.activation(tw[:], ds[t][:], COPY, scale=2.0)
+            twice.append(tw)
+
+        for t in range(PACK):
+            pa = keep.tile([P, W], F32, name="pa%d" % t, tag=pa_tags[t], align_bytes=64)
+            nc.vector.tensor_copy(pa[:], aw[t][:].indirect(n1_t[:]))
+            pb = keep.tile([P, W], F32, name="pb%d" % t, tag=pb_tags[t], align_bytes=64)
+            nc.vector.tensor_scalar(pb[:], aw[t][:].indirect(n2_t[:]), -0.5, 0.0, MULT, ADD)
+            pab.append((pa, pb))
+            if t > 0:
+                fold(t - 1)
+        fold(PACK - 1)
+
+        zf = keep.tile([P, PACK, H], F32, name="zf", tag="zf", align_bytes=64)
+        zw = keep.tile([P, PACK, P, PACK], BF16, name="zw", tag="zw", align_bytes=64)
+        for h in range(2):
+            cols = slice(h * HALF, (h + 1) * HALF)
+            for t in range(PACK):
+                nc.vector.tensor_tensor(
+                    zf[:, t, cols], ds[t][:].indirect(n3_t[:, 16 * h : 16 * (h + 1)]), twice[t][:, cols], SUB
+                )
+            src = zf[:].rearrange("p j (m u) -> p m j u", u=PACK)
+            dst = zw[:].rearrange("p u m j -> p m j u")
+            if h == 0:
+                nc.scalar.copy(dst[:, 0:64], src[:, 0:64])
+            else:
+                nc.scalar.copy(dst[:, 64:84], src[:, 64:84])
+                nc.vector.tensor_copy(dst[:, 84:128], src[:, 84:128])
+
+        z_c = keep.tile([P, H], U32, name="z_c", align_bytes=64)
+        z_s = keep.tile([P, H], U8, name="z_s", align_bytes=64)
+        for u in range(PACK):
+            cols = slice(u * P, (u + 1) * P)
+            quantize(z_c[:, cols], z_s[:, cols], zw[:, u].rearrange("p m j -> p (m j)"))
+
+        last_page = keep.tile([P, U], F32, name="last_page", tag="zw", align_bytes=64)
+        nc.vector.memset(last_page[:], 0.0)
+        pages.append(last_page)
+
+        cv = []
+        pos = []
+        accs = []
+
+        def plain(u):
+            c = keep.tile([P, N], F32, name="cv%d" % u)
+            nc.scalar.activation(c[:], accs[u][:], COPY, scale=0.0625)
+            cv.append(c)
+
+        for u in range(PACK):
+            cols = slice(u * P, (u + 1) * P)
+            acc = psum.tile([P, N], F32, name="c_acc%d" % u, tag="bank%d" % u)
+            product(acc[:], z_c[:, cols], z_s[:, cols], z2_c[:], z2_s[:])
+            r = keep.tile([P, N], F32, name="pos%d" % u)
+            nc.scalar.activation(r[:], acc[:], RELU, scale=0.0625)
+            pos.append(r)
+            accs.append(acc)
+            if u > 0:
+                plain(u - 1)
+        plain(PACK - 1)
+
+        out_rows = out_0.rearrange("(p u) w -> u p w", u=PACK)
+        negs = []
+
+        def put(u):
+            nc.vector.tensor_tensor(pages[u][:].indirect(n4_t[:]), cv[u][:], negs[u][:], ADD)
+            nc.sync.dma_start(out_rows[u], pages[u][:])
+
+        for u in range(PACK):
+            neg = keep.tile([P, N], F32, name="neg%d" % u)
+            negs.append(neg)
+            for h in range(2):
+                cols = slice(h * HALF, (h + 1) * HALF)
+                nc.vector.tensor_scalar(
+                    neg[:, cols], pos[u][:].indirect(n5_t[:, 16 * h : 16 * (h + 1)]), -1.0, 0.0, MULT, ADD
+                )
+            if u > 0:
+                put(u - 1)
+        put(PACK - 1)
+
+        ow = keep.tile([P, U, PACK], BF16, name="ow", align_bytes=64)
+        for u in range(2):
+            nc.scalar.copy(ow[:, :, u], pages[u][:])
+        nc.scalar.copy(ow[:, :, 2:4], pages[2][:].unsqueeze(2).to_broadcast([P, U, 2]))
+        o_c = keep.tile([P, U], U32, name="o_c", align_bytes=64)
+        o_s = keep.tile([P, U], U8, name="o_s", align_bytes=64)
+        words_out = out_1[0].rearrange("p c r -> p (c r)").bitcast(I32)
+        for g in range(4):
+            cols = slice(g * 256, (g + 1) * 256)
+            if g % 2 == 0:
+                nc.vector.tensor_copy(ow[:, cols, 3], pages[3][:, cols])
+            else:
+                nc.scalar.copy(ow[:, cols, 3], pages[3][:, cols])
+        for g in range(4):
+            cols = slice(g * 256, (g + 1) * 256)
+            quantize(o_c[:, cols], o_s[:, cols], ow[:, cols, :].rearrange("p c j -> p (c j)"))
+            nc.sync.dma_start(words_out[:, cols], o_c[:, cols].bitcast(I32))
+        for q in range(4):
+            nc.sync.dma_start(out_2[0, 4 * q : 4 * q + 4, :].bitcast(I32), o_s[32 * q : 32 * q + 4, :].bitcast(I32))

@@ -38,12 +38,12 @@ def tile_picked_momfolddpagez_none_po_kernel(
             return lst
 
         def load_weight_half(w, h, name):
-            raw = keep.tile([P, PACK, HALF], F32, name=name)
+            raw = keep.tile([P, PACK, HALF], F32, name=name, tag="raw%d" % h)
             nc.sync.dma_start(raw[:], w.rearrange("(p j) c -> p j c", j=PACK)[:, :, h * HALF : (h + 1) * HALF])
             return raw
 
-        def weave(dst, src):
-            nc.scalar.copy(
+        def weave(dst, src, copy=nc.scalar.copy):
+            copy(
                 dst.rearrange("p (c i) j -> p c j i", i=4),
                 src.rearrange("p j (c i) -> p c j i", i=4),
             )
@@ -58,13 +58,11 @@ def tile_picked_momfolddpagez_none_po_kernel(
             )
 
         xs = keep.tile([P, T], U8, name="xs")
-        nc.vector.memset(xs[:].bitcast(I32), 0)
+        nc.gpsimd.memset(xs[:].bitcast(I32), 0)
         offs_t = load_list(offs, "offs_t")
         two_t = load_list(two, "two_t")
-        wa_raw = [load_weight_half(wa, 0, "wa_raw0")]
         for q in range(4):
             nc.sync.dma_start(xs[32 * q : 32 * q + 4, :].bitcast(I32), x_scales[0, 4 * q : 4 * q + 4, :].bitcast(I32))
-        wa_raw.append(load_weight_half(wa, 1, "wa_raw1"))
         xw = keep.tile([P, T], I32, name="xw")
         nc.sync.dma_start(xw[:], x_words[0].rearrange("p c r -> p (c r)").bitcast(I32))
 
@@ -72,6 +70,7 @@ def tile_picked_momfolddpagez_none_po_kernel(
         nc.gpsimd.memset(grow[:], 0.0)
         ident = keep.tile([P, P], F32, name="ident")
         make_identity(nc, ident[:])
+        wa_raw = [load_weight_half(wa, h, "wa_raw%d" % h) for h in range(2)]
         for row, g in ((0, gt), (PACK, gi)):
             nc.sync.dma_start(
                 grow[row : row + PACK, :].rearrange("t (b r) -> t b r", r=8),
@@ -79,14 +78,14 @@ def tile_picked_momfolddpagez_none_po_kernel(
             )
         n1_t = load_list(n1, "n1_t")
         n2_t = load_list(n2, "n2_t")
-        wb_raw = [load_weight_half(wb, h, "wb_raw%d" % h) for h in range(2)]
         n3_t = load_list(n3, "n3_t")
         n5_t = load_list(n5, "n5_t")
         n4_t = load_list(n4, "n4_t")
 
-        pages = [keep.tile([P, U], F32, name="page%d" % t) for t in range(PACK - 1)]
-        for page in pages:
-            nc.vector.memset(page[:], 0.0)
+        pages = [keep.tile([P, U], F32, name="page%d" % t) for t in range(PACK)]
+        for t in range(PACK):
+            engine = nc.vector if t < 2 else nc.gpsimd
+            engine.memset(pages[t][:].bitcast(I32), 0)
 
         def pick_scales(lst, name):
             got = keep.tile([P, S], U8, name=name + "_got")
@@ -98,8 +97,8 @@ def tile_picked_momfolddpagez_none_po_kernel(
             )
             return dealt
 
-        def pick_words(lst, name):
-            dealt = keep.tile([P, S], U32, name=name, align_bytes=64)
+        def pick_words(lst, name, tag):
+            dealt = keep.tile([P, S], U32, name=name, tag=tag, align_bytes=64)
             nc.vector.tensor_copy(
                 dealt[:].rearrange("p (t b r) -> p b t r", t=PACK, r=8), xw[:].bitcast(U32).indirect(lst[:])
             )
@@ -107,44 +106,85 @@ def tile_picked_momfolddpagez_none_po_kernel(
 
         xa_s = pick_scales(offs_t, "xa_s")
         xb_s = pick_scales(two_t, "xb_s")
+        xa_c = pick_words(offs_t, "xa_c", "xa_c")
 
         wa_c = keep.tile([P, H], U32, name="wa_c", align_bytes=64)
         wa_s = keep.tile([P, H], U8, name="wa_s", align_bytes=64)
         for h in range(2):
-            woven = keep.tile([P, HALF, PACK], BF16, name="wa_w%d" % h, align_bytes=64)
-            weave(woven[:], wa_raw[h][:])
+            woven = keep.tile([P, HALF, PACK], BF16, name="wa_w%d" % h, tag="wa_w%d" % h, align_bytes=64)
+            if h == 0:
+                weave(woven[:], wa_raw[h][:])
+            else:
+                weave(woven[:, 0:104], wa_raw[h][:, :, 0:104])
+                weave(woven[:, 104:HALF], wa_raw[h][:, :, 104:HALF], nc.vector.tensor_copy)
             cols = slice(h * HALF, (h + 1) * HALF)
             quantize(wa_c[:, cols], wa_s[:, cols], woven[:].rearrange("p c j -> p (c j)"))
 
-        xa_c = pick_words(offs_t, "xa_c")
-        xb_c = pick_words(two_t, "xb_c")
+
+        xb_c = pick_words(two_t, "xb_c", "wa_w1")
 
         gT = psum.tile([P, P], F32, name="gT", tag="bank7")
         nc.tensor.transpose(gT[:], grow[:], ident[:])
         gcol = keep.tile([P, 2 * PACK], F32, name="gcol")
-        nc.scalar.activation(gcol[:, 0:PACK], gT[:, 0:PACK], COPY, scale=-0.5)
-        nc.scalar.copy(gcol[:, PACK : 2 * PACK], gT[:, PACK : 2 * PACK])
+        nc.scalar.copy(gcol[:], gT[:, 0 : 2 * PACK])
 
-        ds = []
-        aw = []
-        a_accs = []
+        def banked_products(first_banks, l_codes, l_scales, r_codes, r_scales, name):
+            parts = []
+            for t in range(PACK):
+                rows = slice(t * P, (t + 1) * P)
+                spans = [(slice(0, HALF), 0), (slice(HALF, 2 * HALF), PACK)] if t == 0 else [(slice(0, 2 * HALF), t)]
+                mine = []
+                for cols, bank in spans:
+                    acc = psum.tile([P, cols.stop - cols.start], F32, name="%s%d_%d" % (name, t, bank), tag="bank%d" % bank)
+                    product(acc[:], l_codes[:, rows], l_scales[:, rows], r_codes[:, cols], r_scales[:, cols])
+                    mine.append((cols, acc))
+                parts.append(mine)
+            return parts
 
-        def second(t):
-            d = keep.tile([P, H], F32, name="ds%d" % t)
-            nc.scalar.activation(d[:], a_accs[t][:], COPY, scale=gcol[:, t : t + 1])
-            ds.append(d)
+        def empty_into(dst, parts, func, scale):
+            for cols, acc in parts:
+                nc.scalar.activation(dst[:, cols], acc[:], func, scale=scale)
 
-        for t in range(PACK):
-            acc = psum.tile([P, H], F32, name="a_acc%d" % t, tag="bank%d" % t)
-            cols = slice(t * P, (t + 1) * P)
-            product(acc[:], xa_c[:, cols], xa_s[:, cols], wa_c[:], wa_s[:])
-            d = keep.tile([P, H], F32, name="aw%d" % t)
-            nc.scalar.activation(d[:], acc[:], COPY, scale=gcol[:, t : t + 1])
-            aw.append(d)
-            a_accs.append(acc)
-            if t > 0:
-                second(t - 1)
-        second(PACK - 1)
+        def empty(parts, func, scale, name):
+            dst = keep.tile([P, 2 * HALF], F32, name=name)
+            empty_into(dst[:], parts, func, scale)
+            return dst
+
+        a_parts = banked_products(0, xa_c, xa_s, wa_c, wa_s, "a_acc")
+        wb_raw = [load_weight_half(wb, h, "wb_raw%d" % h) for h in range(2)]
+        aw, ds, pab, halves = [], [], [], []
+
+        def window_a(t):
+            aw.append(empty(a_parts[t], COPY, gcol[:, t : t + 1], "aw%d" % t))
+
+        def base_a(t):
+            ds.append(empty(a_parts[t], COPY, gcol[:, t : t + 1], "ds%d" % t))
+
+        def fetch(t, pa_tag, pb_tag):
+            pa = keep.tile([P, W], F32, name="pa%d" % t, tag=pa_tag, align_bytes=64)
+            pb = keep.tile([P, W], F32, name="pb%d" % t, tag=pb_tag, align_bytes=64)
+            nc.vector.tensor_scalar(pb[:], aw[t][:].indirect(n2_t[:]), -0.5, 0.0, MULT, ADD)
+            nc.vector.tensor_copy(pa[:], aw[t][:].indirect(n1_t[:]))
+            pab.append((pa, pb))
+
+        def fold(t):
+            nc.vector.tensor_tensor(ds[t][:].indirect(n2_t[:]), pab[t][0][:], pab[t][1][:], ADD)
+
+        def halve(t):
+            hv = keep.tile([P, H], F32, name="half%d" % t, tag="half%d" % t, align_bytes=64)
+            nc.scalar.activation(hv[:], ds[t][:], COPY, scale=-0.5)
+            halves.append(hv)
+
+        window_a(0)
+        window_a(1)
+        base_a(0)
+        window_a(2)
+        base_a(1)
+        fetch(0, "pa0", "pb0")
+        fetch(1, "pa1", "pb1")
+        fold(0)
+        fetch(2, "pa2", "pb2")
+        fold(1)
 
         wb_c = keep.tile([P, N], U32, name="wb_c", align_bytes=64)
         wb_s = keep.tile([P, N], U8, name="wb_s", align_bytes=64)
@@ -153,6 +193,15 @@ def tile_picked_momfolddpagez_none_po_kernel(
             weave(woven[:], wb_raw[h][:])
             cols = slice(h * HALF, (h + 1) * HALF)
             quantize(wb_c[:, cols], wb_s[:, cols], woven[:].rearrange("p c j -> p (c j)"))
+        window_a(3)
+        base_a(2)
+        base_a(3)
+        halve(0)
+        halve(1)
+        fetch(3, "zf", "wb_w1")
+        fold(2)
+        fold(3)
+
         z2f = keep.tile([P, PACK, N], F32, name="z2f")
         for t in range(PACK):
             acc = psum.tile([P, N], F32, name="b_acc%d" % t, tag="bank%d" % (PACK + t))
@@ -160,47 +209,26 @@ def tile_picked_momfolddpagez_none_po_kernel(
             product(acc[:], xb_c[:, cols], xb_s[:, cols], wb_c[:], wb_s[:])
             nc.scalar.activation(z2f[:, t, :], acc[:], COPY, scale=gcol[:, PACK + t : PACK + t + 1])
         z2w = keep.tile([P, N, PACK], BF16, name="z2w", align_bytes=64)
-        weave(z2w[:], z2f[:])
-        z2_c = keep.tile([P, N], U32, name="z2_c", align_bytes=64)
-        z2_s = keep.tile([P, N], U8, name="z2_s", align_bytes=64)
-        quantize(z2_c[:], z2_s[:], z2w[:].rearrange("p c j -> p (c j)"))
-
-        pa_tags = ["pa0", "pa1", "pa2", "zf"]
-        pb_tags = ["pb0", "pb1", "pb2", "wb_w1"]
-        twice = []
-        pab = []
-
-        def fold(t):
-            nc.vector.tensor_tensor(ds[t][:].indirect(n2_t[:]), pab[t][0][:], pab[t][1][:], ADD)
-            tw = keep.tile([P, H], F32, name="twice%d" % t)
-            nc.scalar.activation(tw[:], ds[t][:], COPY, scale=2.0)
-            twice.append(tw)
-
-        for t in range(PACK):
-            pa = keep.tile([P, W], F32, name="pa%d" % t, tag=pa_tags[t], align_bytes=64)
-            nc.vector.tensor_copy(pa[:], aw[t][:].indirect(n1_t[:]))
-            pb = keep.tile([P, W], F32, name="pb%d" % t, tag=pb_tags[t], align_bytes=64)
-            nc.vector.tensor_scalar(pb[:], aw[t][:].indirect(n2_t[:]), -0.5, 0.0, MULT, ADD)
-            pab.append((pa, pb))
-            if t > 0:
-                fold(t - 1)
-        fold(PACK - 1)
+        for h in range(2):
+            halve(2 + h)
+            cols = slice(h * HALF, (h + 1) * HALF)
+            weave(z2w[:, cols], z2f[:, :, cols])
 
         zf = keep.tile([P, PACK, H], F32, name="zf", tag="zf", align_bytes=64)
-        zw = keep.tile([P, PACK, P, PACK], BF16, name="zw", tag="zw", align_bytes=64)
-        for h in range(2):
-            cols = slice(h * HALF, (h + 1) * HALF)
+        zw = keep.tile([P, PACK, P, PACK], BF16, name="zw", align_bytes=64)
+        for lo, hi in ((0, 256), (256, 384), (384, 512)):
             for t in range(PACK):
                 nc.vector.tensor_tensor(
-                    zf[:, t, cols], ds[t][:].indirect(n3_t[:, 16 * h : 16 * (h + 1)]), twice[t][:, cols], SUB
+                    zf[:, t, lo:hi], halves[t][:].indirect(n3_t[:, lo // 16 : hi // 16]), ds[t][:, lo:hi], ADD
                 )
-            src = zf[:].rearrange("p j (m u) -> p m j u", u=PACK)
-            dst = zw[:].rearrange("p u m j -> p m j u")
-            if h == 0:
-                nc.scalar.copy(dst[:, 0:64], src[:, 0:64])
-            else:
-                nc.scalar.copy(dst[:, 64:84], src[:, 64:84])
-                nc.vector.tensor_copy(dst[:, 84:128], src[:, 84:128])
+            nc.scalar.copy(
+                zw[:].rearrange("p u m j -> p m j u")[:, lo // PACK : hi // PACK],
+                zf[:].rearrange("p j (m u) -> p m j u", u=PACK)[:, lo // PACK : hi // PACK],
+            )
+
+        z2_c = keep.tile([P, N], U32, name="z2_c", tag="half3", align_bytes=64)
+        z2_s = keep.tile([P, N], U8, name="z2_s", align_bytes=64)
+        quantize(z2_c[:], z2_s[:], z2w[:].rearrange("p c j -> p (c j)"))
 
         z_c = keep.tile([P, H], U32, name="z_c", align_bytes=64)
         z_s = keep.tile([P, H], U8, name="z_s", align_bytes=64)
@@ -208,54 +236,37 @@ def tile_picked_momfolddpagez_none_po_kernel(
             cols = slice(u * P, (u + 1) * P)
             quantize(z_c[:, cols], z_s[:, cols], zw[:, u].rearrange("p m j -> p (m j)"))
 
-        last_page = keep.tile([P, U], F32, name="last_page", tag="zw", align_bytes=64)
-        nc.vector.memset(last_page[:], 0.0)
-        pages.append(last_page)
 
-        cv = []
-        pos = []
-        accs = []
-
-        def plain(u):
-            c = keep.tile([P, N], F32, name="cv%d" % u)
-            nc.scalar.activation(c[:], accs[u][:], COPY, scale=0.0625)
-            cv.append(c)
-
-        for u in range(PACK):
-            cols = slice(u * P, (u + 1) * P)
-            acc = psum.tile([P, N], F32, name="c_acc%d" % u, tag="bank%d" % u)
-            product(acc[:], z_c[:, cols], z_s[:, cols], z2_c[:], z2_s[:])
-            r = keep.tile([P, N], F32, name="pos%d" % u)
-            nc.scalar.activation(r[:], acc[:], RELU, scale=0.0625)
-            pos.append(r)
-            accs.append(acc)
+        c_parts = banked_products(0, z_c, z_s, z2_c, z2_s, "c_acc")
+        pos = [keep.tile([P, N if u == 0 else 2 * N], F32, name="pos%d" % u) for u in range(PACK)]
+        last_cv = keep.tile([P, N], F32, name="last_cv")
+        cv = [pos[u + 1][:, N : 2 * N] for u in range(PACK - 1)] + [last_cv[:]]
+        for u in range(PACK + 1):
+            if u < PACK:
+                empty_into(pos[u][:, 0:N], c_parts[u], RELU, 0.0625)
             if u > 0:
-                plain(u - 1)
-        plain(PACK - 1)
+                empty_into(cv[u - 1], c_parts[u - 1], COPY, 0.0625)
 
         out_rows = out_0.rearrange("(p u) w -> u p w", u=PACK)
         negs = []
-
-        def put(u):
-            nc.vector.tensor_tensor(pages[u][:].indirect(n4_t[:]), cv[u][:], negs[u][:], ADD)
-            nc.sync.dma_start(out_rows[u], pages[u][:])
-
-        for u in range(PACK):
-            neg = keep.tile([P, N], F32, name="neg%d" % u)
-            negs.append(neg)
-            for h in range(2):
-                cols = slice(h * HALF, (h + 1) * HALF)
-                nc.vector.tensor_scalar(
-                    neg[:, cols], pos[u][:].indirect(n5_t[:, 16 * h : 16 * (h + 1)]), -1.0, 0.0, MULT, ADD
-                )
+        for u in range(PACK + 1):
+            if u < PACK:
+                neg = keep.tile([P, N], F32, name="neg%d" % u)
+                negs.append(neg)
+                for lo, hi in ((0, HALF), (HALF, N)) if u == 0 else ((0, N),):
+                    nc.vector.tensor_scalar(
+                        neg[:, lo:hi], pos[u][:].indirect(n5_t[:, lo // 16 : hi // 16]), -1.0, 0.0, MULT, ADD
+                    )
             if u > 0:
-                put(u - 1)
-        put(PACK - 1)
+                nc.vector.tensor_tensor(pages[u - 1][:].indirect(n4_t[:]), cv[u - 1], negs[u - 1][:], ADD)
+                nc.sync.dma_start(out_rows[u - 1], pages[u - 1][:])
 
         ow = keep.tile([P, U, PACK], BF16, name="ow", align_bytes=64)
         for u in range(2):
             nc.scalar.copy(ow[:, :, u], pages[u][:])
-        nc.scalar.copy(ow[:, :, 2:4], pages[2][:].unsqueeze(2).to_broadcast([P, U, 2]))
+        for g in (0, 2, 1, 3):
+            cols = slice(g * 256, (g + 1) * 256)
+            nc.scalar.copy(ow[:, cols, 2:4], pages[2][:, cols].unsqueeze(2).to_broadcast([P, 256, 2]))
         o_c = keep.tile([P, U], U32, name="o_c", align_bytes=64)
         o_s = keep.tile([P, U], U8, name="o_s", align_bytes=64)
         words_out = out_1[0].rearrange("p c r -> p (c r)").bitcast(I32)
@@ -270,4 +281,5 @@ def tile_picked_momfolddpagez_none_po_kernel(
             quantize(o_c[:, cols], o_s[:, cols], ow[:, cols, :].rearrange("p c j -> p (c j)"))
             nc.sync.dma_start(words_out[:, cols], o_c[:, cols].bitcast(I32))
         for q in range(4):
-            nc.sync.dma_start(out_2[0, 4 * q : 4 * q + 4, :].bitcast(I32), o_s[32 * q : 32 * q + 4, :].bitcast(I32))
+            queue = nc.sync if q < 2 else nc.scalar
+            queue.dma_start(out_2[0, 4 * q : 4 * q + 4, :].bitcast(I32), o_s[32 * q : 32 * q + 4, :].bitcast(I32))

@@ -152,23 +152,26 @@ def tile_picked_momfolddpagez_none_po_kernel(
 
         a_parts = banked_products(0, xa_c, xa_s, wa_c, wa_s, "a_acc")
         wb_raw = [load_weight_half(wb, h, "wb_raw%d" % h) for h in range(2)]
-        aw, ds, pab, halves = [], [], [], []
+        ds, pas, pbs, halves = [], [], [], []
 
         def window_a(t):
-            aw.append(empty(a_parts[t], COPY, gcol[:, t : t + 1], "aw%d" % t))
-
-        def base_a(t):
             ds.append(empty(a_parts[t], COPY, gcol[:, t : t + 1], "ds%d" % t))
 
         def fetch(t, pa_tag, pb_tag):
             pa = keep.tile([P, W], F32, name="pa%d" % t, tag=pa_tag, align_bytes=64)
             pb = keep.tile([P, W], F32, name="pb%d" % t, tag=pb_tag, align_bytes=64)
-            nc.vector.tensor_scalar(pb[:], aw[t][:].indirect(n2_t[:]), -0.5, 0.0, MULT, ADD)
-            nc.vector.tensor_copy(pa[:], aw[t][:].indirect(n1_t[:]))
-            pab.append((pa, pb))
+            nc.vector.tensor_copy(pb[:], ds[t][:].indirect(n2_t[:]))
+            nc.vector.tensor_copy(pa[:], ds[t][:].indirect(n1_t[:]))
+            pas.append(pa)
+            pbs.append(pb)
+
+        def weigh(t):
+            less = keep.tile([P, W], F32, name="less%d" % t)
+            nc.scalar.activation(less[:], pbs[t][:], COPY, scale=-0.5)
+            pbs[t] = less
 
         def fold(t):
-            nc.vector.tensor_tensor(ds[t][:].indirect(n2_t[:]), pab[t][0][:], pab[t][1][:], ADD)
+            nc.vector.tensor_tensor(ds[t][:].indirect(n2_t[:]), pas[t][:], pbs[t][:], ADD)
 
         def halve(t):
             hv = keep.tile([P, H], F32, name="half%d" % t, tag="half%d" % t, align_bytes=64)
@@ -177,11 +180,12 @@ def tile_picked_momfolddpagez_none_po_kernel(
 
         window_a(0)
         window_a(1)
-        base_a(0)
-        window_a(2)
-        base_a(1)
         fetch(0, "pa0", "pb0")
+        weigh(0)
+        window_a(2)
         fetch(1, "pa1", "pb1")
+        weigh(1)
+        window_a(3)
         fold(0)
         fetch(2, "pa2", "pb2")
         fold(1)
@@ -193,12 +197,11 @@ def tile_picked_momfolddpagez_none_po_kernel(
             weave(woven[:], wb_raw[h][:])
             cols = slice(h * HALF, (h + 1) * HALF)
             quantize(wb_c[:, cols], wb_s[:, cols], woven[:].rearrange("p c j -> p (c j)"))
-        window_a(3)
-        base_a(2)
-        base_a(3)
+        weigh(2)
         halve(0)
         halve(1)
         fetch(3, "zf", "wb_w1")
+        weigh(3)
         fold(2)
         fold(3)
 
@@ -208,36 +211,60 @@ def tile_picked_momfolddpagez_none_po_kernel(
             cols = slice(t * P, (t + 1) * P)
             product(acc[:], xb_c[:, cols], xb_s[:, cols], wb_c[:], wb_s[:])
             nc.scalar.activation(z2f[:, t, :], acc[:], COPY, scale=gcol[:, PACK + t : PACK + t + 1])
-        z2w = keep.tile([P, N, PACK], BF16, name="z2w", align_bytes=64)
+        z2w = []
         for h in range(2):
             halve(2 + h)
-            cols = slice(h * HALF, (h + 1) * HALF)
-            weave(z2w[:, cols], z2f[:, :, cols])
+            woven = keep.tile([P, HALF, PACK], BF16, name="z2w%d" % h, tag=("late", "z2w1")[h], align_bytes=64)
+            weave(woven[:], z2f[:, :, h * HALF : (h + 1) * HALF])
+            z2w.append(woven)
 
-        zf = keep.tile([P, PACK, H], F32, name="zf", tag="zf", align_bytes=64)
+        def quantize_z2(h, tag):
+            codes = keep.tile([P, HALF], U32, name="z2_c%d" % h, tag=tag, align_bytes=64)
+            scales = keep.tile([P, HALF], U8, name="z2_s%d" % h, align_bytes=64)
+            quantize(codes[:], scales[:], z2w[h][:].rearrange("p c j -> p (c j)"))
+            return codes, scales
+
         zw = keep.tile([P, PACK, P, PACK], BF16, name="zw", align_bytes=64)
-        for lo, hi in ((0, 256), (256, 384), (384, 512)):
+        dealt = zw[:].rearrange("p u m j -> p m j u")
+        z2q = []
+        for h in range(2):
+            zf = keep.tile([P, PACK, HALF], F32, name="zf%d" % h, tag=("zf", "late")[h], align_bytes=64)
             for t in range(PACK):
                 nc.vector.tensor_tensor(
-                    zf[:, t, lo:hi], halves[t][:].indirect(n3_t[:, lo // 16 : hi // 16]), ds[t][:, lo:hi], ADD
+                    zf[:, t, :],
+                    halves[t][:].indirect(n3_t[:, 16 * h : 16 * (h + 1)]),
+                    ds[t][:, h * HALF : (h + 1) * HALF],
+                    ADD,
                 )
-            nc.scalar.copy(
-                zw[:].rearrange("p u m j -> p m j u")[:, lo // PACK : hi // PACK],
-                zf[:].rearrange("p j (m u) -> p m j u", u=PACK)[:, lo // PACK : hi // PACK],
-            )
-
-        z2_c = keep.tile([P, N], U32, name="z2_c", tag="half3", align_bytes=64)
-        z2_s = keep.tile([P, N], U8, name="z2_s", align_bytes=64)
-        quantize(z2_c[:], z2_s[:], z2w[:].rearrange("p c j -> p (c j)"))
+            src = zf[:].rearrange("p j (m u) -> p m j u", u=PACK)
+            if h == 0:
+                nc.scalar.copy(dealt[:, 0:64], src)
+                z2q.append(quantize_z2(0, "z2_c0"))
+            else:
+                nc.scalar.copy(dealt[:, 64:80], src[:, 0:16])
+                nc.vector.tensor_copy(dealt[:, 80:128], src[:, 16:64])
 
         z_c = keep.tile([P, H], U32, name="z_c", align_bytes=64)
         z_s = keep.tile([P, H], U8, name="z_s", align_bytes=64)
         for u in range(PACK):
             cols = slice(u * P, (u + 1) * P)
             quantize(z_c[:, cols], z_s[:, cols], zw[:, u].rearrange("p m j -> p (m j)"))
+            if u == 0:
+                z2q.append(quantize_z2(1, "late"))
 
-
-        c_parts = banked_products(0, z_c, z_s, z2_c, z2_s, "c_acc")
+        c_parts = []
+        for u in range(PACK):
+            rows = slice(u * P, (u + 1) * P)
+            if u == 0:
+                accs = [psum.tile([P, HALF], F32, name="c_acc0_%d" % h, tag="bank%d" % (PACK * h)) for h in range(2)]
+                outs = [acc[:] for acc in accs]
+                c_parts.append([(slice(h * HALF, (h + 1) * HALF), accs[h]) for h in range(2)])
+            else:
+                acc = psum.tile([P, N], F32, name="c_acc%d" % u, tag="bank%d" % u)
+                outs = [acc[:, h * HALF : (h + 1) * HALF] for h in range(2)]
+                c_parts.append([(slice(0, N), acc)])
+            for h in range(2):
+                product(outs[h], z_c[:, rows], z_s[:, rows], z2q[h][0][:], z2q[h][1][:])
         pos = [keep.tile([P, N if u == 0 else 2 * N], F32, name="pos%d" % u) for u in range(PACK)]
         last_cv = keep.tile([P, N], F32, name="last_cv")
         cv = [pos[u + 1][:, N : 2 * N] for u in range(PACK - 1)] + [last_cv[:]]

from contextlib import ExitStack

import concourse.mybir as mybir
from concourse.masks import make_identity

K, T, S, N, H, W, U = 512, 2048, 512, 512, 512, 256, 1024
FLOPS = 3 * 2 * 512 * 512 * 512

F32 = mybir.dt.float32
BF16 = mybir.dt.bfloat16
I32 = mybir.dt.int32
U32 = mybir.dt.uint32
U16 = mybir.dt.uint16
U8 = mybir.dt.uint8
FP8X4 = mybir.dt.float8_e4m3fn_x4
MULT = mybir.AluOpType.mult
ADD = mybir.AluOpType.add
SUB = mybir.AluOpType.subtract
COPY = mybir.ActivationFunctionType.Copy
RELU = mybir.ActivationFunctionType.Relu

P = 128
PACK = 4
HALF = 256


def tile_picked_momfolddpagez_none_po_kernel(
    tc, x_words, x_scales, wa, wb, gt, gi, offs, two, n1, n2, n3, n4, n5, out_0, out_1, out_2
):
    nc = tc.nc
    with ExitStack() as ctx:
        keep = ctx.enter_context(tc.tile_pool(name="keep", bufs=1))
        psum = ctx.enter_context(tc.psum_pool(name="psum", bufs=1))

        def load_list(src, name):
            lst = keep.tile([P, src.shape[1]], U16, name=name)
            nc.sync.dma_start(lst[:], src)
            return lst

        def load_weight_half(w, h, name):
            raw = keep.tile([P, PACK, HALF], F32, name=name, tag="raw%d" % h)
            nc.sync.dma_start(raw[:], w.rearrange("(p j) c -> p j c", j=PACK)[:, :, h * HALF : (h + 1) * HALF])
            return raw

        def weave(dst, src, copy=nc.scalar.copy):
            copy(
                dst.rearrange("p (c i) j -> p c j i", i=4),
                src.rearrange("p j (c i) -> p c j i", i=4),
            )

        def quantize(codes, scales, src):
            nc.vector.quantize_mx(out=codes.bitcast(FP8X4), scales=scales, in_=src)

        def product(acc, l_codes, l_scales, r_codes, r_scales):
            nc.tensor.matmul_mx(
                out=acc, lhsT=l_codes.bitcast(FP8X4), lhsT_scale=l_scales,
                rhs=r_codes.bitcast(FP8X4), rhs_scale=r_scales, start=True, stop=True,
            )

        xs = keep.tile([P, T], U8, name="xs")
        nc.gpsimd.memset(xs[:].bitcast(I32), 0)
        offs_t = load_list(offs, "offs_t")
        two_t = load_list(two, "two_t")
        for q in range(4):
            nc.sync.dma_start(xs[32 * q : 32 * q + 4, :].bitcast(I32), x_scales[0, 4 * q : 4 * q + 4, :].bitcast(I32))
        xw = keep.tile([P, T], I32, name="xw")
        nc.sync.dma_start(xw[:], x_words[0].rearrange("p c r -> p (c r)").bitcast(I32))

        grow = keep.tile([P, P], F32, name="grow")
        nc.gpsimd.memset(grow[:], 0.0)
        ident = keep.tile([P, P], F32, name="ident")
        make_identity(nc, ident[:])
        wa_raw = [load_weight_half(wa, h, "wa_raw%d" % h) for h in range(2)]
        for row, g in ((0, gt), (PACK, gi)):
            nc.sync.dma_start(
                grow[row : row + PACK, :].rearrange("t (b r) -> t b r", r=8),
                g.rearrange("(b t r) one -> t b (r one)", t=PACK, r=8),
            )
        n1_t = load_list(n1, "n1_t")
        n2_t = load_list(n2, "n2_t")
        n3_t = load_list(n3, "n3_t")
        n5_t = load_list(n5, "n5_t")
        n4_t = load_list(n4, "n4_t")

        pages = [keep.tile([P, U], F32, name="page%d" % t) for t in range(PACK)]
        for t in range(PACK):
            engine = nc.vector if t < 2 else nc.gpsimd
            engine.memset(pages[t][:].bitcast(I32), 0)

        def pick_scales(lst, name):
            got = keep.tile([P, S], U8, name=name + "_got")
            nc.vector.tensor_copy(got[:], xs[:].indirect(lst[:]))
            dealt = keep.tile([P, S], U8, name=name, align_bytes=64)
            nc.vector.tensor_copy(
                dealt[:].bitcast(I32).rearrange("p (t b w) -> p t b w", t=PACK, w=2),
                got[:].bitcast(I32).rearrange("p (b t w) -> p t b w", t=PACK, w=2),
            )
            return dealt

        def pick_words(lst, name, tag):
            dealt = keep.tile([P, S], U32, name=name, tag=tag, align_bytes=64)
            nc.vector.tensor_copy(
                dealt[:].rearrange("p (t b r) -> p b t r", t=PACK, r=8), xw[:].bitcast(U32).indirect(lst[:])
            )
            return dealt

        xa_s = pick_scales(offs_t, "xa_s")
        xb_s = pick_scales(two_t, "xb_s")
        xa_c = pick_words(offs_t, "xa_c", "xa_c")

        wa_c = keep.tile([P, H], U32, name="wa_c", align_bytes=64)
        wa_s = keep.tile([P, H], U8, name="wa_s", align_bytes=64)
        for h in range(2):
            woven = keep.tile([P, HALF, PACK], BF16, name="wa_w%d" % h, tag="wa_w%d" % h, align_bytes=64)
            if h == 0:
                weave(woven[:], wa_raw[h][:])
            else:
                weave(woven[:, 0:104], wa_raw[h][:, :, 0:104])
                weave(woven[:, 104:HALF], wa_raw[h][:, :, 104:HALF], nc.vector.tensor_copy)
            cols = slice(h * HALF, (h + 1) * HALF)
            quantize(wa_c[:, cols], wa_s[:, cols], woven[:].rearrange("p c j -> p (c j)"))


        xb_c = pick_words(two_t, "xb_c", "wa_w1")

        gT = psum.tile([P, P], F32, name="gT", tag="bank7")
        nc.tensor.transpose(gT[:], grow[:], ident[:])
        gcol = keep.tile([P, 2 * PACK], F32, name="gcol")
        nc.scalar.copy(gcol[:], gT[:, 0 : 2 * PACK])

        def banked_products(first_banks, l_codes, l_scales, r_codes, r_scales, name):
            parts = []
            for t in range(PACK):
                rows = slice(t * P, (t + 1) * P)
                spans = [(slice(0, HALF), 0), (slice(HALF, 2 * HALF), PACK)] if t == 0 else [(slice(0, 2 * HALF), t)]
                mine = []
                for cols, bank in spans:
                    acc = psum.tile([P, cols.stop - cols.start], F32, name="%s%d_%d" % (name, t, bank), tag="bank%d" % bank)
                    product(acc[:], l_codes[:, rows], l_scales[:, rows], r_codes[:, cols], r_scales[:, cols])
                    mine.append((cols, acc))
                parts.append(mine)
            return parts

        def empty_into(dst, parts, func, scale):
            for cols, acc in parts:
                nc.scalar.activation(dst[:, cols], acc[:], func, scale=scale)

        def empty(parts, func, scale, name):
            dst = keep.tile([P, 2 * HALF], F32, name=name)
            empty_into(dst[:], parts, func, scale)
            return dst

        a_parts = banked_products(0, xa_c, xa_s, wa_c, wa_s, "a_acc")
        wb_raw = [load_weight_half(wb, h, "wb_raw%d" % h) for h in range(2)]
        ds, pas, pbs, halves = [], [], [], []

        def window_a(t):
            ds.append(empty(a_parts[t], COPY, gcol[:, t : t + 1], "ds%d" % t))

        def fetch(t, pa_tag, pb_tag):
            pa = keep.tile([P, W], F32, name="pa%d" % t, tag=pa_tag, align_bytes=64)
            pb = keep.tile([P, W], F32, name="pb%d" % t, tag=pb_tag, align_bytes=64)
            nc.vector.tensor_copy(pb[:], ds[t][:].indirect(n2_t[:]))
            nc.vector.tensor_copy(pa[:], ds[t][:].indirect(n1_t[:]))
            pas.append(pa)
            pbs.append(pb)

        def weigh(t):
            less = keep.tile([P, W], F32, name="less%d" % t)
            nc.scalar.activation(less[:], pbs[t][:], COPY, scale=-0.5)
            pbs[t] = less

        def fold(t):
            nc.vector.tensor_tensor(ds[t][:].indirect(n2_t[:]), pas[t][:], pbs[t][:], ADD)

        def halve(t):
            hv = keep.tile([P, H], F32, name="half%d" % t, tag="half%d" % t, align_bytes=64)
            nc.scalar.activation(hv[:], ds[t][:], COPY, scale=-0.5)
            halves.append(hv)

        window_a(0)
        window_a(1)
        fetch(0, "pa0", "pb0")
        weigh(0)
        window_a(2)
        fetch(1, "pa1", "pb1")
        weigh(1)
        window_a(3)
        fold(0)
        fetch(2, "pa2", "pb2")
        fold(1)

        wb_c = keep.tile([P, N], U32, name="wb_c", align_bytes=64)
        wb_s = keep.tile([P, N], U8, name="wb_s", align_bytes=64)
        for h in range(2):
            woven = keep.tile([P, HALF, PACK], BF16, name="wb_w%d" % h, tag="wb_w%d" % h, align_bytes=64)
            weave(woven[:], wb_raw[h][:])
            cols = slice(h * HALF, (h + 1) * HALF)
            quantize(wb_c[:, cols], wb_s[:, cols], woven[:].rearrange("p c j -> p (c j)"))
        weigh(2)
        halve(0)
        halve(1)
        fetch(3, "zf", "wb_w1")
        weigh(3)
        fold(2)
        fold(3)

        z2f = keep.tile([P, PACK, N], F32, name="z2f")
        for t in range(PACK):
            acc = psum.tile([P, N], F32, name="b_acc%d" % t, tag="bank%d" % (PACK + t))
            cols = slice(t * P, (t + 1) * P)
            product(acc[:], xb_c[:, cols], xb_s[:, cols], wb_c[:], wb_s[:])
            nc.scalar.activation(z2f[:, t, :], acc[:], COPY, scale=gcol[:, PACK + t : PACK + t + 1])
        z2w = []
        for h in range(2):
            halve(2 + h)
            woven = keep.tile([P, HALF, PACK], BF16, name="z2w%d" % h, tag=("late", "z2w1")[h], align_bytes=64)
            weave(woven[:], z2f[:, :, h * HALF : (h + 1) * HALF])
            z2w.append(woven)

        def quantize_z2(h, tag):
            codes = keep.tile([P, HALF], U32, name="z2_c%d" % h, tag=tag, align_bytes=64)
            scales = keep.tile([P, HALF], U8, name="z2_s%d" % h, align_bytes=64)
            quantize(codes[:], scales[:], z2w[h][:].rearrange("p c j -> p (c j)"))
            return codes, scales

        zw = keep.tile([P, PACK, P, PACK], BF16, name="zw", align_bytes=64)
        dealt = zw[:].rearrange("p u m j -> p m j u")
        z2q = []
        for h in range(2):
            zf = keep.tile([P, PACK, HALF], F32, name="zf%d" % h, tag=("zf", "late")[h], align_bytes=64)
            for t in range(PACK):
                nc.vector.tensor_tensor(
                    zf[:, t, :],
                    halves[t][:].indirect(n3_t[:, 16 * h : 16 * (h + 1)]),
                    ds[t][:, h * HALF : (h + 1) * HALF],
                    ADD,
                )
            src = zf[:].rearrange("p j (m u) -> p m j u", u=PACK)
            if h == 0:
                nc.scalar.copy(dealt[:, 0:64], src)
                z2q.append(quantize_z2(0, "z2_c0"))
            else:
                nc.scalar.copy(dealt[:, 64:80], src[:, 0:16])
                nc.vector.tensor_copy(dealt[:, 80:128], src[:, 16:64])

        z_c = keep.tile([P, H], U32, name="z_c", align_bytes=64)
        z_s = keep.tile([P, H], U8, name="z_s", align_bytes=64)
        for u in range(PACK):
            cols = slice(u * P, (u + 1) * P)
            quantize(z_c[:, cols], z_s[:, cols], zw[:, u].rearrange("p m j -> p (m j)"))
            if u == 0:
                z2q.append(quantize_z2(1, "late"))

        c_parts = []
        for u in range(PACK):
            rows = slice(u * P, (u + 1) * P)
            if u == 0:
                accs = [psum.tile([P, HALF], F32, name="c_acc0_%d" % h, tag="bank%d" % (PACK * h)) for h in range(2)]
                outs = [acc[:] for acc in accs]
                c_parts.append([(slice(h * HALF, (h + 1) * HALF), accs[h]) for h in range(2)])
            else:
                acc = psum.tile([P, N], F32, name="c_acc%d" % u, tag="bank%d" % u)
                outs = [acc[:, h * HALF : (h + 1) * HALF] for h in range(2)]
                c_parts.append([(slice(0, N), acc)])
            for h in range(2):
                product(outs[h], z_c[:, rows], z_s[:, rows], z2q[h][0][:], z2q[h][1][:])
        pos = [keep.tile([P, N if u == 0 else 2 * N], F32, name="pos%d" % u) for u in range(PACK)]
        last_cv = keep.tile([P, N], F32, name="last_cv")
        cv = [pos[u + 1][:, N : 2 * N] for u in range(PACK - 1)] + [last_cv[:]]
        for u in range(PACK + 1):
            if u < PACK:
                empty_into(pos[u][:, 0:N], c_parts[u], RELU, 0.0625)
            if u > 0:
                empty_into(cv[u - 1], c_parts[u - 1], COPY, 0.0625)

        out_rows = out_0.rearrange("(p u) w -> u p w", u=PACK)
        negs = []
        for u in range(PACK + 1):
            if u < PACK:
                neg = keep.tile([P, N], F32, name="neg%d" % u)
                negs.append(neg)
                for lo, hi in ((0, HALF), (HALF, N)) if u == 0 else ((0, N),):
                    nc.vector.tensor_scalar(
                        neg[:, lo:hi], pos[u][:].indirect(n5_t[:, lo // 16 : hi // 16]), -1.0, 0.0, MULT, ADD
                    )
            if u > 0:
                nc.vector.tensor_tensor(pages[u - 1][:].indirect(n4_t[:]), cv[u - 1], negs[u - 1][:], ADD)
                nc.sync.dma_start(out_rows[u - 1], pages[u - 1][:])

        ow = keep.tile([P, U, PACK], BF16, name="ow", align_bytes=64)
        for u in range(2):
            nc.scalar.copy(ow[:, :, u], pages[u][:])
        for g in (0, 2, 1, 3):
            cols = slice(g * 256, (g + 1) * 256)
            nc.scalar.copy(ow[:, cols, 2:4], pages[2][:, cols].unsqueeze(2).to_broadcast([P, 256, 2]))
        o_c = keep.tile([P, U], U32, name="o_c", align_bytes=64)
        o_s = keep.tile([P, U], U8, name="o_s", align_bytes=64)
        words_out = out_1[0].rearrange("p c r -> p (c r)").bitcast(I32)
        for g in range(4):
            cols = slice(g * 256, (g + 1) * 256)
            if g % 2 == 0:
                nc.vector.tensor_copy(ow[:, cols, 3], pages[3][:, cols])
            else:
                nc.scalar.copy(ow[:, cols, 3], pages[3][:, cols])
        for g in range(4):
            cols = slice(g * 256, (g + 1) * 256)
            quantize(o_c[:, cols], o_s[:, cols], ow[:, cols, :].rearrange("p c j -> p (c j)"))
            nc.sync.dma_start(words_out[:, cols], o_c[:, cols].bitcast(I32))
        for q in range(4):
            queue = nc.sync if q < 2 else nc.scalar
            queue.dma_start(out_2[0, 4 * q : 4 * q + 4, :].bitcast(I32), o_s[32 * q : 32 * q + 4, :].bitcast(I32))
